import numpy as np
import ml_dtypes


def mxq(x, axis, fmt="e4m3"):
    dtype, down = {"e4m3": (ml_dtypes.float8_e4m3fn, 7), "e5m2": (ml_dtypes.float8_e5m2, 14)}[fmt]
    v = np.moveaxis(np.asarray(x, np.float32).astype(ml_dtypes.bfloat16).astype(np.float64), axis, -1)
    blocks = v.reshape(v.shape[:-1] + (-1, 32))
    amax = np.abs(blocks).max(-1, keepdims=True)
    byte = np.maximum(np.where(amax > 0, np.frexp(amax)[1] - 1 + 127, 0) - down, 1)
    scale = np.exp2(byte - 127.0)
    codes = (blocks / scale).astype(np.float32).astype(dtype).astype(np.float64)
    return np.moveaxis((codes * scale).reshape(v.shape), -1, axis)


WIDE = False


def mx_kscale(k):
    if not WIDE:
        return np.ones(k)
    levels = np.array([10, -10, 5, -5, 0])
    if k % 512:
        return np.exp2(np.random.permutation(np.resize(levels, k // 32))).repeat(32)
    a = np.empty((k // 512, 16))
    for p in range(k // 512):
        a[p, :8] = np.random.permutation(np.resize(levels, 8))
        for g in range(8):
            far = levels[np.abs(levels - a[p, g]) >= 10]
            a[p, g + 8] = far[np.random.randint(len(far))]
    return np.exp2(a.ravel()).repeat(32)


def f64(x):
    return np.asarray(x).astype(np.float64)


def striped(idx):
    return np.tile(idx.reshape(-1, 16).T, (8, 1)).astype(np.uint16)


def unstriped(offs):
    return offs[:16].T.reshape(-1).astype(np.int64)


def pack_weight(w):
    k, n = w.shape
    w = f64(np.asarray(w, np.float32).astype(ml_dtypes.bfloat16)).reshape(k // 32, 32, n)
    amax = np.abs(w).max(1)
    byte = np.clip(np.where(amax > 0, np.frexp(amax)[1] - 1 + 127 - 7, 1), 1, 254)
    scaled = (w * np.exp2(127.0 - byte)[:, None, :]).reshape(k, n).astype(np.float32)
    words = np.ascontiguousarray(scaled.reshape(k // 512, 128, 4, n).transpose(0, 1, 3, 2)).astype(ml_dtypes.float8_e4m3fn).view(np.uint8)
    return words, np.ascontiguousarray(byte.astype(np.uint8).reshape(k // 512, 16, n))


def unpack_weight(words, scales):
    g, p, n, _ = words.shape
    vals = np.ascontiguousarray(words).view(ml_dtypes.float8_e4m3fn).astype(np.float64) * np.repeat(np.exp2(scales.astype(np.float64) - 127.0), 8, axis=1)[..., None]
    return vals.transpose(0, 1, 3, 2).reshape(g * 512, n)


def planes(y):
    n, m = y.shape
    v = y.astype(np.float32).astype(ml_dtypes.bfloat16).astype(np.float64).reshape(n // 32, 32, m)
    top = np.abs(v).max(1)
    byte = np.clip(np.where(top > 0, np.frexp(top)[1] - 1 + 127 - 7, 1), 1, 254)
    codes = (v * np.exp2(127.0 - byte)[:, None, :]).reshape(n, m).astype(np.float32).astype(ml_dtypes.float8_e4m3fn).view(np.uint8)
    words = codes.reshape(n // 512, 128, 4, m).transpose(0, 1, 3, 2)
    return np.ascontiguousarray(words), np.ascontiguousarray(byte.astype(np.uint8).reshape(n // 512, 16, m))


def silu(v):
    return v / (1.0 + np.exp(-np.maximum(v, -700.0)))


K, T, S, V, H, N = 512, 4096, 1024, 256, 512, 512


def setup_inputs():
    n = np.random.standard_normal
    s = mx_kscale(K)[:, None]
    u = mx_kscale(H)
    packed_xT = pack_weight(n((K, T)) * s)
    packed_w2 = pack_weight(n((K, N)) / np.sqrt(K) / s)
    packed_w3 = pack_weight(n((H, N)) / np.sqrt(H) / u[:, None])
    return {
        "x_words": packed_xT[0],
        "x_scales": packed_xT[1],
        "w1": (n((K, H)) / np.sqrt(K) / s * u).astype(np.float32),
        "w2_words": packed_w2[0],
        "w2_scales": packed_w2[1],
        "w3_words": packed_w3[0],
        "w3_scales": packed_w3[1],
        "offs": striped(np.random.permutation(T)[:S]),
    }


def reference(x_words, x_scales, w1, w2_words, w2_scales, w3_words, w3_scales, offs):
    xq = unpack_weight(x_words, x_scales)[:, unstriped(offs)]
    w1q = mxq(f64(w1), 0, "e4m3")
    h0 = w1q.T @ xq[:, :V]
    w2q = unpack_weight(w2_words, w2_scales)
    e1 = w2q.T @ xq[:, V:2 * V]
    e2 = w2q.T @ xq[:, 2 * V:3 * V]
    e3 = w2q.T @ xq[:, 3 * V:4 * V]
    h1 = w1q.T @ xq[:, V:2 * V]
    h2 = w1q.T @ xq[:, 2 * V:3 * V]
    z = h0 * e1 + h0 * e2 + h0 * e3 + h1 * e2 + h1 * e3 + h2 * e3
    out_0 = silu(unpack_weight(w3_words, w3_scales).T @ mxq(z, 0, "e4m3"))
    return (out_0,) + planes(out_0)

@@ -1,0 +1,177 @@
+from contextlib import ExitStack
+
+import concourse.mybir as mybir
+
+K, T, S, V, H, N = 512, 4096, 1024, 256, 512, 512
+FLOPS = 7 * 2 * 512 * 512 * 256
+
+F32 = mybir.dt.float32
+BF16 = mybir.dt.bfloat16
+I32 = mybir.dt.int32
+U32 = mybir.dt.uint32
+U16 = mybir.dt.uint16
+U8 = mybir.dt.uint8
+FP8X4 = mybir.dt.float8_e4m3fn_x4
+ADD = mybir.AluOpType.add
+MULT = mybir.AluOpType.mult
+SILU = mybir.ActivationFunctionType.Silu
+
+P = 128
+PACK = 4
+FIELDS = 4
+HALF = 128
+BANKS = 8
+
+
+def tile_picked_zfibi_silu_po_kernel(
+    tc, x_words, x_scales, w1, w2_words, w2_scales, w3_words, w3_scales, offs, out_0, out_1, out_2
+):
+    nc = tc.nc
+    with ExitStack() as ctx:
+        keep = ctx.enter_context(tc.tile_pool(name="keep", bufs=1))
+        psum = ctx.enter_context(tc.psum_pool(name="psum", bufs=1))
+
+        def words_of(packed):
+            return packed[0].rearrange("p c r -> p (c r)").bitcast(I32)
+
+        def load_scale_rows(queue, plane, rows):
+            for q in range(4):
+                queue.dma_start(out=plane[32 * q : 32 * q + 4, :].bitcast(I32), in_=rows[0, 4 * q : 4 * q + 4, :].bitcast(I32))
+
+        offsets = keep.tile([P, S // 16], U16)
+        nc.sync.dma_start(offsets[:], offs)
+
+        table_scales = keep.tile([P, T], U8, align_bytes=64)
+        nc.vector.memset(table_scales[:].bitcast(I32), 0)
+        w2_scales_raw = keep.tile([P, H], U8, align_bytes=64)
+        nc.vector.memset(w2_scales_raw[:].bitcast(I32), 0)
+        w3_scales_raw = keep.tile([P, N], U8, align_bytes=64)
+        nc.vector.memset(w3_scales_raw[:].bitcast(I32), 0)
+
+        w1_raw = keep.tile([P, PACK, H], F32, tag="staging", align_bytes=64)
+        nc.sync.dma_start(out=w1_raw[:], in_=w1.rearrange("(p j) c -> p j c", j=PACK))
+        table_words = keep.tile([P, T], U32, align_bytes=64)
+        nc.sync.dma_start(out=table_words[:].bitcast(I32), in_=words_of(x_words))
+        w2_words_raw = keep.tile([P, H], U32, align_bytes=64)
+        nc.sync.dma_start(out=w2_words_raw[:].bitcast(I32), in_=words_of(w2_words))
+        load_scale_rows(nc.scalar, table_scales, x_scales)
+        load_scale_rows(nc.gpsimd, w2_scales_raw, w2_scales)
+        load_scale_rows(nc.gpsimd, w3_scales_raw, w3_scales)
+
+        picked_scales = keep.tile([P, S], U8, align_bytes=64)
+        nc.vector.tensor_copy(picked_scales[:], table_scales[:].indirect(offsets[:]))
+
+        w1_bf = keep.tile([P, PACK, P, PACK], BF16, align_bytes=64)
+        w1_codes = keep.tile([P, H], U32, align_bytes=64)
+        w1_plane = keep.tile([P, H], U8, align_bytes=64)
+        for u in range(2):
+            ts = slice(2 * u, 2 * u + 2)
+            nc.scalar.copy(
+                out=w1_bf[:, ts].rearrange("p t m j -> p m t j"),
+                in_=w1_raw[:].rearrange("p j (m t) -> p m t j", t=PACK)[:, :, ts, :],
+            )
+            cols = slice(2 * P * u, 2 * P * (u + 1))
+            nc.vector.quantize_mx(
+                out=w1_codes[:, cols].bitcast(FP8X4),
+                scales=w1_plane[:, cols],
+                in_=w1_bf[:, ts].rearrange("p t m j -> p (t m j)"),
+            )
+
+        w3_words_raw = keep.tile([P, N], U32, tag="staging", align_bytes=64)
+        nc.sync.dma_start(out=w3_words_raw[:].bitcast(I32), in_=words_of(w3_words))
+
+        def deal(copy, dealt, raw):
+            copy(out=dealt[:].rearrange("p (t m) -> p m t", t=PACK), in_=raw[:].rearrange("p (m t) -> p m t", t=PACK))
+
+        w2_plane = keep.tile([P, H], U8, align_bytes=64)
+        deal(nc.vector.tensor_copy, w2_plane, w2_scales_raw)
+        w2_codes = keep.tile([P, H], U32, align_bytes=64)
+        deal(nc.scalar.copy, w2_codes, w2_words_raw)
+        w3_plane = keep.tile([P, N], U8, align_bytes=64)
+        deal(nc.gpsimd.tensor_copy, w3_plane, w3_scales_raw)
+
+        picked = []
+        for d in range(FIELDS):
+            field = keep.tile([P, V], U32, name=f"field{d}", align_bytes=64)
+            nc.vector.tensor_copy(field[:], table_words[:].indirect(offsets[:, d * V // 16 : (d + 1) * V // 16]))
+            picked.append(field)
+
+        banks_used = []
+
+        def product(codes, plane, moving):
+            bank = psum.tile([P, PACK, HALF], F32, name=f"bank{len(banks_used) % BANKS}")
+            banks_used.append(bank)
+            for t in range(PACK):
+                cols = slice(P * t, P * (t + 1))
+                for n, (rhs, rhs_scale) in enumerate(moving):
+                    nc.tensor.matmul_mx(
+                        out=bank[:, t, :],
+                        lhsT=codes[:, cols].bitcast(FP8X4),
+                        lhsT_scale=plane[:, cols],
+                        rhs=rhs.bitcast(FP8X4),
+                        rhs_scale=rhs_scale,
+                        start=(n == 0),
+                        stop=(n == len(moving) - 1),
+                    )
+            return bank
+
+        def woven(bank):
+            return bank[:].rearrange("p t v -> p v t")
+
+        z_ops = []
+        for half in range(V // HALF):
+            def field_half(d):
+                first = HALF * half
+                return picked[d][:, first : first + HALF], picked_scales[:, V * d + first : V * d + first + HALF]
+
+            def f32_tile(name):
+                return keep.tile([P, HALF, PACK], F32, name=f"{name}_{half}", align_bytes=64)
+
+            h0 = product(w1_codes, w1_plane, [field_half(0)])
+            h0_sb = f32_tile("h0")
+            nc.scalar.copy(out=h0_sb[:], in_=woven(h0))
+            h1 = product(w1_codes, w1_plane, [field_half(1)])
+            h01 = f32_tile("h01")
+            nc.vector.tensor_tensor(h01[:], woven(h1), h0_sb[:], ADD)
+            e1 = product(w2_codes, w2_plane, [field_half(1)])
+            p01 = f32_tile("p01")
+            nc.vector.tensor_tensor(p01[:], woven(e1), h0_sb[:], MULT)
+            h2 = product(w1_codes, w1_plane, [field_half(2)])
+            h2_sb = f32_tile("h2")
+            nc.scalar.copy(out=h2_sb[:], in_=woven(h2))
+            e3 = product(w2_codes, w2_plane, [field_half(3)])
+            p23 = f32_tile("p23")
+            nc.vector.tensor_tensor(p23[:], woven(e3), h2_sb[:], MULT)
+            e23 = product(w2_codes, w2_plane, [field_half(2), field_half(3)])
+            pmid = f32_tile("pmid")
+            nc.vector.tensor_tensor(pmid[:], woven(e23), h01[:], MULT)
+            pair = f32_tile("pair")
+            nc.vector.tensor_tensor(pair[:], p01[:], p23[:], ADD)
+            z_bf = keep.tile([P, HALF, PACK], BF16, name=f"z_bf_{half}", align_bytes=64)
+            nc.vector.tensor_tensor(z_bf[:], pair[:], pmid[:], ADD)
+            z_codes = keep.tile([P, HALF], U32, name=f"z_codes_{half}", align_bytes=64)
+            z_plane = keep.tile([P, HALF], U8, name=f"z_plane_{half}", align_bytes=64)
+            nc.vector.quantize_mx(out=z_codes[:].bitcast(FP8X4), scales=z_plane[:], in_=z_bf[:].rearrange("p v t -> p (v t)"))
+            z_ops.append((z_codes[:], z_plane[:]))
+
+        w3_codes = keep.tile([P, N], U32, align_bytes=64)
+        deal(nc.scalar.copy, w3_codes, w3_words_raw)
+
+        y_codes = keep.tile([P, V], U32, align_bytes=64)
+        y_plane = keep.tile([P, V], U8, align_bytes=64)
+        out_rows = out_0.rearrange("(p t) v -> p t v", t=PACK)
+        for half in range(V // HALF):
+            cols = slice(HALF * half, HALF * (half + 1))
+            pre = product(w3_codes, w3_plane, [z_ops[half]])
+            y = keep.tile([P, PACK, HALF], F32, name=f"y_{half}", align_bytes=64)
+            nc.scalar.activation(out=y[:], in_=pre[:], func=SILU)
+            nc.sync.dma_start(out=out_rows[:, :, cols], in_=y[:])
+            y_bf = keep.tile([P, HALF, PACK], BF16, name=f"y_bf_{half}", align_bytes=64)
+            nc.vector.tensor_copy(out=y_bf[:], in_=y[:].rearrange("p t v -> p v t"))
+            nc.vector.quantize_mx(
+                out=y_codes[:, cols].bitcast(FP8X4), scales=y_plane[:, cols], in_=y_bf[:].rearrange("p v t -> p (v t)")
+            )
+            nc.sync.dma_start(out=words_of(out_1)[:, cols], in_=y_codes[:, cols].bitcast(I32))
+        for q in range(4):
+            queue = nc.scalar if q % 2 else nc.sync
+            queue.dma_start(out=out_2[0, 4 * q : 4 * q + 4, :].bitcast(I32), in_=y_plane[32 * q : 32 * q + 4, :].bitcast(I32))

@@ -1,6 +1,7 @@
 from contextlib import ExitStack
 
 import concourse.mybir as mybir
+from concourse.masks import make_identity
 
 K, T, S, V, H, N = 512, 4096, 1024, 256, 512, 512
 FLOPS = 7 * 2 * 512 * 512 * 256
@@ -35,60 +36,60 @@ def tile_picked_zfibi_silu_po_kernel(
             return packed[0].rearrange("p c r -> p (c r)").bitcast(I32)
 
         def load_scale_rows(queue, plane, rows):
-            for q in range(4):
-                queue.dma_start(out=plane[32 * q : 32 * q + 4, :].bitcast(I32), in_=rows[0, 4 * q : 4 * q + 4, :].bitcast(I32))
+            for r in range(4):
+                queue.dma_start(out=plane[r:P:32, :].bitcast(I32), in_=rows[0, r:16:4, :].bitcast(I32))
 
         offsets = keep.tile([P, S // 16], U16)
         nc.sync.dma_start(offsets[:], offs)
 
-        table_scales = keep.tile([P, T], U8, align_bytes=64)
+        table_scales = keep.tile([P, T], U8, tag="scales", align_bytes=64)
         nc.vector.memset(table_scales[:].bitcast(I32), 0)
         w2_scales_raw = keep.tile([P, H], U8, align_bytes=64)
-        nc.vector.memset(w2_scales_raw[:].bitcast(I32), 0)
+        nc.gpsimd.memset(w2_scales_raw[:].bitcast(I32), 0)
+        zeros = keep.tile([P, N // 4], I32, tag="table", align_bytes=64)
+        nc.vector.memset(zeros[:], 0)
         w3_scales_raw = keep.tile([P, N], U8, align_bytes=64)
-        nc.vector.memset(w3_scales_raw[:].bitcast(I32), 0)
+        nc.vector.tensor_copy(w3_scales_raw[:].bitcast(I32), zeros[:])
 
         w1_raw = keep.tile([P, PACK, H], F32, tag="staging", align_bytes=64)
         nc.sync.dma_start(out=w1_raw[:], in_=w1.rearrange("(p j) c -> p j c", j=PACK))
-        table_words = keep.tile([P, T], U32, align_bytes=64)
+        load_scale_rows(nc.sync, table_scales, x_scales)
+        table_words = keep.tile([P, T], U32, tag="table", align_bytes=64)
         nc.sync.dma_start(out=table_words[:].bitcast(I32), in_=words_of(x_words))
-        w2_words_raw = keep.tile([P, H], U32, align_bytes=64)
-        nc.sync.dma_start(out=w2_words_raw[:].bitcast(I32), in_=words_of(w2_words))
-        load_scale_rows(nc.scalar, table_scales, x_scales)
         load_scale_rows(nc.gpsimd, w2_scales_raw, w2_scales)
-        load_scale_rows(nc.gpsimd, w3_scales_raw, w3_scales)
+        load_scale_rows(nc.sync, w3_scales_raw, w3_scales)
 
         picked_scales = keep.tile([P, S], U8, align_bytes=64)
         nc.vector.tensor_copy(picked_scales[:], table_scales[:].indirect(offsets[:]))
 
-        w1_bf = keep.tile([P, PACK, P, PACK], BF16, align_bytes=64)
+        identity = keep.tile([P, P], F32)
+        make_identity(nc, identity[:])
+
+        warm = keep.tile([P, 1], F32)
+        nc.scalar.activation(out=warm[:], in_=identity[:, 0:1], func=SILU)
+
+        w1_bf = keep.tile([P, H, PACK], BF16, align_bytes=64)
         w1_codes = keep.tile([P, H], U32, align_bytes=64)
         w1_plane = keep.tile([P, H], U8, align_bytes=64)
-        for u in range(2):
-            ts = slice(2 * u, 2 * u + 2)
+        for first in (0, H // 2):
+            cols = slice(first, first + H // 2)
             nc.scalar.copy(
-                out=w1_bf[:, ts].rearrange("p t m j -> p m t j"),
-                in_=w1_raw[:].rearrange("p j (m t) -> p m t j", t=PACK)[:, :, ts, :],
+                out=w1_bf[:, cols].rearrange("p (c i) j -> p c j i", i=4),
+                in_=w1_raw[:, :, cols].rearrange("p j (c i) -> p c j i", i=4),
             )
-            cols = slice(2 * P * u, 2 * P * (u + 1))
             nc.vector.quantize_mx(
                 out=w1_codes[:, cols].bitcast(FP8X4),
                 scales=w1_plane[:, cols],
-                in_=w1_bf[:, ts].rearrange("p t m j -> p (t m j)"),
+                in_=w1_bf[:, cols].rearrange("p c j -> p (c j)"),
             )
 
-        w3_words_raw = keep.tile([P, N], U32, tag="staging", align_bytes=64)
+        w2_codes = keep.tile([P, H], U32, tag="staging", align_bytes=64)
+        nc.sync.dma_start(out=w2_codes[:].bitcast(I32), in_=words_of(w2_words))
+        w3_words_raw = keep.tile([P, N], U32, tag="scales", align_bytes=64)
         nc.sync.dma_start(out=w3_words_raw[:].bitcast(I32), in_=words_of(w3_words))
 
         def deal(copy, dealt, raw):
             copy(out=dealt[:].rearrange("p (t m) -> p m t", t=PACK), in_=raw[:].rearrange("p (m t) -> p m t", t=PACK))
-
-        w2_plane = keep.tile([P, H], U8, align_bytes=64)
-        deal(nc.vector.tensor_copy, w2_plane, w2_scales_raw)
-        w2_codes = keep.tile([P, H], U32, align_bytes=64)
-        deal(nc.scalar.copy, w2_codes, w2_words_raw)
-        w3_plane = keep.tile([P, N], U8, align_bytes=64)
-        deal(nc.gpsimd.tensor_copy, w3_plane, w3_scales_raw)
 
         picked = []
         for d in range(FIELDS):
@@ -96,82 +97,99 @@ def tile_picked_zfibi_silu_po_kernel(
             nc.vector.tensor_copy(field[:], table_words[:].indirect(offsets[:, d * V // 16 : (d + 1) * V // 16]))
             picked.append(field)
 
-        banks_used = []
+        w3_plane = keep.tile([P, N], U8, align_bytes=64)
+        deal(nc.vector.tensor_copy, w3_plane, w3_scales_raw)
 
-        def product(codes, plane, moving):
-            bank = psum.tile([P, PACK, HALF], F32, name=f"bank{len(banks_used) % BANKS}")
-            banks_used.append(bank)
-            for t in range(PACK):
-                cols = slice(P * t, P * (t + 1))
-                for n, (rhs, rhs_scale) in enumerate(moving):
-                    nc.tensor.matmul_mx(
-                        out=bank[:, t, :],
-                        lhsT=codes[:, cols].bitcast(FP8X4),
-                        lhsT_scale=plane[:, cols],
-                        rhs=rhs.bitcast(FP8X4),
-                        rhs_scale=rhs_scale,
-                        start=(n == 0),
-                        stop=(n == len(moving) - 1),
-                    )
-            return bank
+        def projection(bank_number, codes, plane, fields, half):
+            bank = psum.tile([P, H], F32, name=f"bank{bank_number}")
+            first = HALF * half
+            for n, d in enumerate(fields):
+                nc.tensor.matmul_mx(
+                    out=bank[:],
+                    lhsT=picked[d][:, first : first + HALF].bitcast(FP8X4),
+                    lhsT_scale=picked_scales[:, V * d + first : V * d + first + HALF],
+                    rhs=codes[:].bitcast(FP8X4),
+                    rhs_scale=plane[:],
+                    start=(n == 0),
+                    stop=(n == len(fields) - 1),
+                )
+            return bank[:].rearrange("v (p t) -> v t p", t=PACK)
 
-        def woven(bank):
-            return bank[:].rearrange("p t v -> p v t")
+        def f32_tile(name, half):
+            return keep.tile([P, PACK, P], F32, name=f"{name}_{half}", align_bytes=64)
 
-        z_ops = []
+        terms = []
         for half in range(V // HALF):
-            def field_half(d):
-                first = HALF * half
-                return picked[d][:, first : first + HALF], picked_scales[:, V * d + first : V * d + first + HALF]
-
-            def f32_tile(name):
-                return keep.tile([P, HALF, PACK], F32, name=f"{name}_{half}", align_bytes=64)
-
-            h0 = product(w1_codes, w1_plane, [field_half(0)])
-            h0_sb = f32_tile("h0")
-            nc.scalar.copy(out=h0_sb[:], in_=woven(h0))
-            h1 = product(w1_codes, w1_plane, [field_half(1)])
-            h01 = f32_tile("h01")
-            nc.vector.tensor_tensor(h01[:], woven(h1), h0_sb[:], ADD)
-            e1 = product(w2_codes, w2_plane, [field_half(1)])
-            p01 = f32_tile("p01")
-            nc.vector.tensor_tensor(p01[:], woven(e1), h0_sb[:], MULT)
-            h2 = product(w1_codes, w1_plane, [field_half(2)])
-            h2_sb = f32_tile("h2")
-            nc.scalar.copy(out=h2_sb[:], in_=woven(h2))
-            e3 = product(w2_codes, w2_plane, [field_half(3)])
-            p23 = f32_tile("p23")
-            nc.vector.tensor_tensor(p23[:], woven(e3), h2_sb[:], MULT)
-            e23 = product(w2_codes, w2_plane, [field_half(2), field_half(3)])
-            pmid = f32_tile("pmid")
-            nc.vector.tensor_tensor(pmid[:], woven(e23), h01[:], MULT)
-            pair = f32_tile("pair")
-            nc.vector.tensor_tensor(pair[:], p01[:], p23[:], ADD)
-            z_bf = keep.tile([P, HALF, PACK], BF16, name=f"z_bf_{half}", align_bytes=64)
-            nc.vector.tensor_tensor(z_bf[:], pair[:], pmid[:], ADD)
-            z_codes = keep.tile([P, HALF], U32, name=f"z_codes_{half}", align_bytes=64)
-            z_plane = keep.tile([P, HALF], U8, name=f"z_plane_{half}", align_bytes=64)
-            nc.vector.quantize_mx(out=z_codes[:].bitcast(FP8X4), scales=z_plane[:], in_=z_bf[:].rearrange("p v t -> p (v t)"))
-            z_ops.append((z_codes[:], z_plane[:]))
+            bank_of = [(6 * half + n) % BANKS for n in range(6)]
+            h0 = f32_tile("h0", half)
+            nc.scalar.copy(out=h0[:], in_=projection(bank_of[0], w1_codes, w1_plane, [0], half))
+            h01 = f32_tile("h01", half)
+            nc.vector.tensor_tensor(h01[:], projection(bank_of[1], w1_codes, w1_plane, [1], half), h0[:], ADD)
+            p01 = f32_tile("p01", half)
+            nc.vector.tensor_tensor(p01[:], projection(bank_of[2], w2_codes, w2_scales_raw, [1], half), h0[:], MULT)
+            h2 = f32_tile("h2", half)
+            nc.scalar.copy(out=h2[:], in_=projection(bank_of[3], w1_codes, w1_plane, [2], half))
+            p23 = f32_tile("p23", half)
+            nc.vector.tensor_tensor(p23[:], projection(bank_of[4], w2_codes, w2_scales_raw, [3], half), h2[:], MULT)
+            pmid = f32_tile("pmid", half)
+            nc.vector.tensor_tensor(pmid[:], projection(bank_of[5], w2_codes, w2_scales_raw, [2, 3], half), h01[:], MULT)
+            terms.append((p01, p23, pmid))
 
         w3_codes = keep.tile([P, N], U32, align_bytes=64)
         deal(nc.scalar.copy, w3_codes, w3_words_raw)
+
+        z_ops = []
+        for half in range(V // HALF):
+            z_sum = psum.tile([P, PACK, HALF], F32, name=f"bank{4 + half}")
+            for n, term in enumerate(terms[half]):
+                for t in range(PACK):
+                    nc.tensor.matmul(
+                        z_sum[:, t, :],
+                        lhsT=term[:, t, :],
+                        rhs=identity[:],
+                        is_transpose=True,
+                        start=(n == 0 and t == 0),
+                        stop=(n == 2 and t == PACK - 1),
+                    )
+            z_bf = keep.tile([P, HALF, PACK], BF16, name=f"z_bf_{half}", align_bytes=64)
+            nc.scalar.copy(out=z_bf[:], in_=z_sum[:].rearrange("p t v -> p v t"))
+            z_codes = keep.tile([P, HALF], U32, name=f"z_codes_{half}", align_bytes=64)
+            z_plane = keep.tile([P, HALF], U8, name=f"z_plane_{half}", align_bytes=64)
+            nc.vector.quantize_mx(out=z_codes[:].bitcast(FP8X4), scales=z_plane[:], in_=z_bf[:].rearrange("p v t -> p (v t)"))
+            z_ops.append((z_codes, z_plane))
 
         y_codes = keep.tile([P, V], U32, align_bytes=64)
         y_plane = keep.tile([P, V], U8, align_bytes=64)
         out_rows = out_0.rearrange("(p t) v -> p t v", t=PACK)
         for half in range(V // HALF):
             cols = slice(HALF * half, HALF * (half + 1))
-            pre = product(w3_codes, w3_plane, [z_ops[half]])
+            z_codes, z_plane = z_ops[half]
+            pre = psum.tile([P, PACK, HALF], F32, name=f"bank{6 + half}")
+            for t in range(PACK):
+                nc.tensor.matmul_mx(
+                    out=pre[:, t, :],
+                    lhsT=w3_codes[:, P * t : P * (t + 1)].bitcast(FP8X4),
+                    lhsT_scale=w3_plane[:, P * t : P * (t + 1)],
+                    rhs=z_codes[:].bitcast(FP8X4),
+                    rhs_scale=z_plane[:],
+                    start=True,
+                    stop=True,
+                )
             y = keep.tile([P, PACK, HALF], F32, name=f"y_{half}", align_bytes=64)
-            nc.scalar.activation(out=y[:], in_=pre[:], func=SILU)
-            nc.sync.dma_start(out=out_rows[:, :, cols], in_=y[:])
             y_bf = keep.tile([P, HALF, PACK], BF16, name=f"y_bf_{half}", align_bytes=64)
-            nc.vector.tensor_copy(out=y_bf[:], in_=y[:].rearrange("p t v -> p v t"))
-            nc.vector.quantize_mx(
-                out=y_codes[:, cols].bitcast(FP8X4), scales=y_plane[:, cols], in_=y_bf[:].rearrange("p v t -> p (v t)")
-            )
+            step = HALF // (1 + half)
+            for first in range(0, HALF, step):
+                part = slice(first, first + step)
+                nc.scalar.activation(out=y[:, :, part], in_=pre[:, :, part], func=SILU)
+                nc.vector.tensor_copy(out=y_bf[:, part], in_=y[:, :, part].rearrange("p t v -> p v t"))
+                planes = slice(HALF * half + first, HALF * half + first + step)
+                nc.vector.quantize_mx(
+                    out=y_codes[:, planes].bitcast(FP8X4),
+                    scales=y_plane[:, planes],
+                    in_=y_bf[:, part].rearrange("p v t -> p (v t)"),
+                )
+            nc.sync.dma_start(out=out_rows[:, :, cols], in_=y[:])
             nc.sync.dma_start(out=words_of(out_1)[:, cols], in_=y_codes[:, cols].bitcast(I32))
-        for q in range(4):
-            queue = nc.scalar if q % 2 else nc.sync
-            queue.dma_start(out=out_2[0, 4 * q : 4 * q + 4, :].bitcast(I32), in_=y_plane[32 * q : 32 * q + 4, :].bitcast(I32))
+        for r in range(4):
+            queue = nc.scalar if r % 2 else nc.sync
+            queue.dma_start(out=out_2[0, r:16:4, :].bitcast(I32), in_=y_plane[r:P:32, :].bitcast(I32))

@@ -83,9 +83,9 @@ def tile_picked_zfibi_silu_po_kernel(
                 in_=w1_bf[:, cols].rearrange("p c j -> p (c j)"),
             )
 
-        w2_codes = keep.tile([P, H], U32, tag="staging", align_bytes=64)
+        w2_codes = keep.tile([P, H], U32, tag="scales", align_bytes=64)
         nc.sync.dma_start(out=w2_codes[:].bitcast(I32), in_=words_of(w2_words))
-        w3_words_raw = keep.tile([P, N], U32, tag="scales", align_bytes=64)
+        w3_words_raw = keep.tile([P, N], U32, tag="staging", align_bytes=64)
         nc.sync.dma_start(out=w3_words_raw[:].bitcast(I32), in_=words_of(w3_words))
 
         def deal(copy, dealt, raw):
@@ -96,9 +96,6 @@ def tile_picked_zfibi_silu_po_kernel(
             field = keep.tile([P, V], U32, name=f"field{d}", align_bytes=64)
             nc.vector.tensor_copy(field[:], table_words[:].indirect(offsets[:, d * V // 16 : (d + 1) * V // 16]))
             picked.append(field)
-
-        w3_plane = keep.tile([P, N], U8, align_bytes=64)
-        deal(nc.vector.tensor_copy, w3_plane, w3_scales_raw)
 
         def projection(bank_number, codes, plane, fields, half):
             bank = psum.tile([P, H], F32, name=f"bank{bank_number}")
@@ -116,15 +113,18 @@ def tile_picked_zfibi_silu_po_kernel(
             return bank[:].rearrange("v (p t) -> v t p", t=PACK)
 
         def f32_tile(name, half):
-            return keep.tile([P, PACK, P], F32, name=f"{name}_{half}", align_bytes=64)
+            return keep.tile([P, PACK, P], F32, name=f"{name}_{half}", tag=f"{name}_{half}", align_bytes=64)
 
         terms = []
         for half in range(V // HALF):
-            bank_of = [(6 * half + n) % BANKS for n in range(6)]
+            bank_of = ((0, 1, 2, 3, 4, 5), (0, 2, 6, 1, 7, 3))[half]
             h0 = f32_tile("h0", half)
             nc.scalar.copy(out=h0[:], in_=projection(bank_of[0], w1_codes, w1_plane, [0], half))
             h01 = f32_tile("h01", half)
-            nc.vector.tensor_tensor(h01[:], projection(bank_of[1], w1_codes, w1_plane, [1], half), h0[:], ADD)
+            if half == 0:
+                nc.vector.tensor_tensor(h01[:], projection(bank_of[1], w1_codes, w1_plane, [1], half), h0[:], ADD)
+            else:
+                nc.scalar.copy(out=h01[:], in_=projection(bank_of[1], w1_codes, w1_plane, [0, 1], half))
             p01 = f32_tile("p01", half)
             nc.vector.tensor_tensor(p01[:], projection(bank_of[2], w2_codes, w2_scales_raw, [1], half), h0[:], MULT)
             h2 = f32_tile("h2", half)
@@ -135,6 +135,8 @@ def tile_picked_zfibi_silu_po_kernel(
             nc.vector.tensor_tensor(pmid[:], projection(bank_of[5], w2_codes, w2_scales_raw, [2, 3], half), h01[:], MULT)
             terms.append((p01, p23, pmid))
 
+        w3_plane = keep.tile([P, N], U8, tag="h01_1", align_bytes=64)
+        deal(nc.vector.tensor_copy, w3_plane, w3_scales_raw)
         w3_codes = keep.tile([P, N], U32, align_bytes=64)
         deal(nc.scalar.copy, w3_codes, w3_words_raw)
 

@@ -44,20 +44,20 @@ def tile_picked_zfibi_silu_po_kernel(
 
         table_scales = keep.tile([P, T], U8, tag="scales", align_bytes=64)
         nc.vector.memset(table_scales[:].bitcast(I32), 0)
-        w2_scales_raw = keep.tile([P, H], U8, align_bytes=64)
-        nc.gpsimd.memset(w2_scales_raw[:].bitcast(I32), 0)
+        w3_scales_raw = keep.tile([P, N], U8, align_bytes=64)
+        nc.gpsimd.memset(w3_scales_raw[:].bitcast(I32), 0)
         zeros = keep.tile([P, N // 4], I32, tag="table", align_bytes=64)
         nc.vector.memset(zeros[:], 0)
-        w3_scales_raw = keep.tile([P, N], U8, align_bytes=64)
-        nc.vector.tensor_copy(w3_scales_raw[:].bitcast(I32), zeros[:])
+        w2_scales_raw = keep.tile([P, H], U8, align_bytes=64)
+        nc.vector.tensor_copy(w2_scales_raw[:].bitcast(I32), zeros[:])
 
         w1_raw = keep.tile([P, PACK, H], F32, tag="staging", align_bytes=64)
         nc.sync.dma_start(out=w1_raw[:], in_=w1.rearrange("(p j) c -> p j c", j=PACK))
         load_scale_rows(nc.sync, table_scales, x_scales)
         table_words = keep.tile([P, T], U32, tag="table", align_bytes=64)
         nc.sync.dma_start(out=table_words[:].bitcast(I32), in_=words_of(x_words))
-        load_scale_rows(nc.gpsimd, w2_scales_raw, w2_scales)
-        load_scale_rows(nc.sync, w3_scales_raw, w3_scales)
+        load_scale_rows(nc.sync, w2_scales_raw, w2_scales)
+        load_scale_rows(nc.gpsimd, w3_scales_raw, w3_scales)
 
         picked_scales = keep.tile([P, S], U8, align_bytes=64)
         nc.vector.tensor_copy(picked_scales[:], table_scales[:].indirect(offsets[:]))

from contextlib import ExitStack

import concourse.mybir as mybir
from concourse.masks import make_identity

K, T, S, V, H, N = 512, 4096, 1024, 256, 512, 512
FLOPS = 7 * 2 * 512 * 512 * 256

F32 = mybir.dt.float32
BF16 = mybir.dt.bfloat16
I32 = mybir.dt.int32
U32 = mybir.dt.uint32
U16 = mybir.dt.uint16
U8 = mybir.dt.uint8
FP8X4 = mybir.dt.float8_e4m3fn_x4
ADD = mybir.AluOpType.add
MULT = mybir.AluOpType.mult
SILU = mybir.ActivationFunctionType.Silu

P = 128
PACK = 4
FIELDS = 4
HALF = 128
BANKS = 8


def tile_picked_zfibi_silu_po_kernel(
    tc, x_words, x_scales, w1, w2_words, w2_scales, w3_words, w3_scales, offs, out_0, out_1, out_2
):
    nc = tc.nc
    with ExitStack() as ctx:
        keep = ctx.enter_context(tc.tile_pool(name="keep", bufs=1))
        psum = ctx.enter_context(tc.psum_pool(name="psum", bufs=1))

        def words_of(packed):
            return packed[0].rearrange("p c r -> p (c r)").bitcast(I32)

        def load_scale_rows(queue, plane, rows):
            for r in range(4):
                queue.dma_start(out=plane[r:P:32, :].bitcast(I32), in_=rows[0, r:16:4, :].bitcast(I32))

        offsets = keep.tile([P, S // 16], U16)
        nc.sync.dma_start(offsets[:], offs)

        table_scales = keep.tile([P, T], U8, tag="scales", align_bytes=64)
        nc.vector.memset(table_scales[:].bitcast(I32), 0)
        w3_scales_raw = keep.tile([P, N], U8, align_bytes=64)
        nc.gpsimd.memset(w3_scales_raw[:].bitcast(I32), 0)
        zeros = keep.tile([P, N // 4], I32, tag="table", align_bytes=64)
        nc.vector.memset(zeros[:], 0)
        w2_scales_raw = keep.tile([P, H], U8, align_bytes=64)
        nc.vector.tensor_copy(w2_scales_raw[:].bitcast(I32), zeros[:])

        w1_raw = keep.tile([P, PACK, H], F32, tag="staging", align_bytes=64)
        nc.sync.dma_start(out=w1_raw[:], in_=w1.rearrange("(p j) c -> p j c", j=PACK))
        load_scale_rows(nc.sync, table_scales, x_scales)
        table_words = keep.tile([P, T], U32, tag="table", align_bytes=64)
        nc.sync.dma_start(out=table_words[:].bitcast(I32), in_=words_of(x_words))
        load_scale_rows(nc.sync, w2_scales_raw, w2_scales)
        load_scale_rows(nc.gpsimd, w3_scales_raw, w3_scales)

        picked_scales = keep.tile([P, S], U8, align_bytes=64)
        nc.vector.tensor_copy(picked_scales[:], table_scales[:].indirect(offsets[:]))

        identity = keep.tile([P, P], F32)
        make_identity(nc, identity[:])

        warm = keep.tile([P, 1], F32)
        nc.scalar.activation(out=warm[:], in_=identity[:, 0:1], func=SILU)

        w1_bf = keep.tile([P, H, PACK], BF16, align_bytes=64)
        w1_codes = keep.tile([P, H], U32, align_bytes=64)
        w1_plane = keep.tile([P, H], U8, align_bytes=64)
        for first in (0, H // 2):
            cols = slice(first, first + H // 2)
            nc.scalar.copy(
                out=w1_bf[:, cols].rearrange("p (c i) j -> p c j i", i=4),
                in_=w1_raw[:, :, cols].rearrange("p j (c i) -> p c j i", i=4),
            )
            nc.vector.quantize_mx(
                out=w1_codes[:, cols].bitcast(FP8X4),
                scales=w1_plane[:, cols],
                in_=w1_bf[:, cols].rearrange("p c j -> p (c j)"),
            )

        w2_codes = keep.tile([P, H], U32, tag="scales", align_bytes=64)
        nc.sync.dma_start(out=w2_codes[:].bitcast(I32), in_=words_of(w2_words))
        w3_words_raw = keep.tile([P, N], U32, tag="staging", align_bytes=64)
        nc.sync.dma_start(out=w3_words_raw[:].bitcast(I32), in_=words_of(w3_words))

        def deal(copy, dealt, raw):
            copy(out=dealt[:].rearrange("p (t m) -> p m t", t=PACK), in_=raw[:].rearrange("p (m t) -> p m t", t=PACK))

        picked = []
        for d in range(FIELDS):
            field = keep.tile([P, V], U32, name=f"field{d}", align_bytes=64)
            nc.vector.tensor_copy(field[:], table_words[:].indirect(offsets[:, d * V // 16 : (d + 1) * V // 16]))
            picked.append(field)

        def projection(bank_number, codes, plane, fields, half):
            bank = psum.tile([P, H], F32, name=f"bank{bank_number}")
            first = HALF * half
            for n, d in enumerate(fields):
                nc.tensor.matmul_mx(
                    out=bank[:],
                    lhsT=picked[d][:, first : first + HALF].bitcast(FP8X4),
                    lhsT_scale=picked_scales[:, V * d + first : V * d + first + HALF],
                    rhs=codes[:].bitcast(FP8X4),
                    rhs_scale=plane[:],
                    start=(n == 0),
                    stop=(n == len(fields) - 1),
                )
            return bank[:].rearrange("v (p t) -> v t p", t=PACK)

        def f32_tile(name, half):
            return keep.tile([P, PACK, P], F32, name=f"{name}_{half}", tag=f"{name}_{half}", align_bytes=64)

        terms = []
        for half in range(V // HALF):
            bank_of = ((0, 1, 2, 3, 4, 5), (0, 2, 6, 1, 7, 3))[half]
            h0 = f32_tile("h0", half)
            nc.scalar.copy(out=h0[:], in_=projection(bank_of[0], w1_codes, w1_plane, [0], half))
            h01 = f32_tile("h01", half)
            if half == 0:
                nc.vector.tensor_tensor(h01[:], projection(bank_of[1], w1_codes, w1_plane, [1], half), h0[:], ADD)
            else:
                nc.scalar.copy(out=h01[:], in_=projection(bank_of[1], w1_codes, w1_plane, [0, 1], half))
            p01 = f32_tile("p01", half)
            nc.vector.tensor_tensor(p01[:], projection(bank_of[2], w2_codes, w2_scales_raw, [1], half), h0[:], MULT)
            h2 = f32_tile("h2", half)
            nc.scalar.copy(out=h2[:], in_=projection(bank_of[3], w1_codes, w1_plane, [2], half))
            p23 = f32_tile("p23", half)
            nc.vector.tensor_tensor(p23[:], projection(bank_of[4], w2_codes, w2_scales_raw, [3], half), h2[:], MULT)
            pmid = f32_tile("pmid", half)
            nc.vector.tensor_tensor(pmid[:], projection(bank_of[5], w2_codes, w2_scales_raw, [2, 3], half), h01[:], MULT)
            terms.append((p01, p23, pmid))

        w3_plane = keep.tile([P, N], U8, tag="h01_1", align_bytes=64)
        deal(nc.vector.tensor_copy, w3_plane, w3_scales_raw)
        w3_codes = keep.tile([P, N], U32, align_bytes=64)
        deal(nc.scalar.copy, w3_codes, w3_words_raw)

        z_ops = []
        for half in range(V // HALF):
            z_sum = psum.tile([P, PACK, HALF], F32, name=f"bank{4 + half}")
            for n, term in enumerate(terms[half]):
                for t in range(PACK):
                    nc.tensor.matmul(
                        z_sum[:, t, :],
                        lhsT=term[:, t, :],
                        rhs=identity[:],
                        is_transpose=True,
                        start=(n == 0 and t == 0),
                        stop=(n == 2 and t == PACK - 1),
                    )
            z_bf = keep.tile([P, HALF, PACK], BF16, name=f"z_bf_{half}", align_bytes=64)
            nc.scalar.copy(out=z_bf[:], in_=z_sum[:].rearrange("p t v -> p v t"))
            z_codes = keep.tile([P, HALF], U32, name=f"z_codes_{half}", align_bytes=64)
            z_plane = keep.tile([P, HALF], U8, name=f"z_plane_{half}", align_bytes=64)
            nc.vector.quantize_mx(out=z_codes[:].bitcast(FP8X4), scales=z_plane[:], in_=z_bf[:].rearrange("p v t -> p (v t)"))
            z_ops.append((z_codes, z_plane))

        y_codes = keep.tile([P, V], U32, align_bytes=64)
        y_plane = keep.tile([P, V], U8, align_bytes=64)
        out_rows = out_0.rearrange("(p t) v -> p t v", t=PACK)
        for half in range(V // HALF):
            cols = slice(HALF * half, HALF * (half + 1))
            z_codes, z_plane = z_ops[half]
            pre = psum.tile([P, PACK, HALF], F32, name=f"bank{6 + half}")
            for t in range(PACK):
                nc.tensor.matmul_mx(
                    out=pre[:, t, :],
                    lhsT=w3_codes[:, P * t : P * (t + 1)].bitcast(FP8X4),
                    lhsT_scale=w3_plane[:, P * t : P * (t + 1)],
                    rhs=z_codes[:].bitcast(FP8X4),
                    rhs_scale=z_plane[:],
                    start=True,
                    stop=True,
                )
            y = keep.tile([P, PACK, HALF], F32, name=f"y_{half}", align_bytes=64)
            y_bf = keep.tile([P, HALF, PACK], BF16, name=f"y_bf_{half}", align_bytes=64)
            step = HALF // (1 + half)
            for first in range(0, HALF, step):
                part = slice(first, first + step)
                nc.scalar.activation(out=y[:, :, part], in_=pre[:, :, part], func=SILU)
                nc.vector.tensor_copy(out=y_bf[:, part], in_=y[:, :, part].rearrange("p t v -> p v t"))
                planes = slice(HALF * half + first, HALF * half + first + step)
                nc.vector.quantize_mx(
                    out=y_codes[:, planes].bitcast(FP8X4),
                    scales=y_plane[:, planes],
                    in_=y_bf[:, part].rearrange("p v t -> p (v t)"),
                )
            nc.sync.dma_start(out=out_rows[:, :, cols], in_=y[:])
            nc.sync.dma_start(out=words_of(out_1)[:, cols], in_=y_codes[:, cols].bitcast(I32))
        for r in range(4):
            queue = nc.scalar if r % 2 else nc.sync
            queue.dma_start(out=out_2[0, r:16:4, :].bitcast(I32), in_=y_plane[r:P:32, :].bitcast(I32))
